import numpy as np
import ml_dtypes


def mxq(x, axis, fmt="e4m3"):
    dtype, down = {"e4m3": (ml_dtypes.float8_e4m3fn, 7), "e5m2": (ml_dtypes.float8_e5m2, 14)}[fmt]
    v = np.moveaxis(np.asarray(x, np.float32).astype(ml_dtypes.bfloat16).astype(np.float64), axis, -1)
    blocks = v.reshape(v.shape[:-1] + (-1, 32))
    amax = np.abs(blocks).max(-1, keepdims=True)
    byte = np.maximum(np.where(amax > 0, np.frexp(amax)[1] - 1 + 127, 0) - down, 1)
    scale = np.exp2(byte - 127.0)
    codes = (blocks / scale).astype(np.float32).astype(dtype).astype(np.float64)
    return np.moveaxis((codes * scale).reshape(v.shape), -1, axis)


WIDE = False


def mx_kscale(k):
    if not WIDE:
        return np.ones(k)
    levels = np.array([30, -30])
    if k % 512:
        return np.exp2(np.random.permutation(np.resize(levels, k // 32))).repeat(32)
    a = np.empty((k // 512, 16))
    for p in range(k // 512):
        a[p, :8] = np.random.permutation(np.resize(levels, 8))
        for g in range(8):
            far = levels[np.abs(levels - a[p, g]) >= 10]
            a[p, g + 8] = far[np.random.randint(len(far))]
    return np.exp2(a.ravel()).repeat(32)


def f64(x):
    return np.asarray(x).astype(np.float64)


def striped(idx):
    return np.tile(np.asarray(idx).reshape(-1, 16).T, (8, 1)).astype(np.uint16)


def unstriped(offs):
    return offs[:16].T.reshape(-1).astype(np.int64)


K, J, N, T, S, V = 256, 1024, 256, 2048, 2048, 2048


def setup_inputs():
    n = np.random.standard_normal
    idx = np.random.permutation(T)[:J]
    idx2 = np.random.permutation(S)[:J]
    idx3 = np.random.permutation(V)[:J]
    fj = mx_kscale(J)
    return {
        "xf": (n((K, T))).astype(np.float32),
        "ra": (np.random.uniform(0.5, 1.5, (1, J)) * fj).astype(np.float32),
        "xb": (n((K, S))).astype(np.float32),
        "gt": (n((N, V)) * np.exp(0.5 * n((1, V)))).astype(np.float32),
        "cb": (np.random.uniform(0.5, 1.5, (J, 1)) / fj[:, None]).astype(np.float32),
        "old": (12.0 * n((K, N))).astype(np.float32),
        "offs": striped(idx),
        "offs2": striped(idx2),
        "offs3": striped(idx3),
    }


def reference(xf, ra, xb, gt, cb, old, offs, offs2, offs3):
    idx = unstriped(offs)
    idx2 = unstriped(offs2)
    idx3 = unstriped(offs3)
    us = f64(xf)[:, idx] * f64(xb)[:, idx2] * f64(ra)
    uj = us.T
    gr1 = f64(gt)[:, idx3].T
    gj = gr1 / (np.max(np.abs(gr1), axis=1, keepdims=True) + 0.2) * f64(cb)
    ujq = mxq(uj, 0, "e4m3")
    gjq = mxq(gj, 0, "e5m2")
    w = ujq.T @ gjq
    y = 0.04 * np.maximum(w, f64(old))
    return y

@@ -1,0 +1,179 @@
+from contextlib import ExitStack
+
+import concourse.mybir as mybir
+from concourse.masks import make_identity
+
+K, J, N, T = 256, 1024, 256, 2048
+FLOPS = 2 * K * J * N
+
+F32 = mybir.dt.float32
+BF16 = mybir.dt.bfloat16
+U32 = mybir.dt.uint32
+U16 = mybir.dt.uint16
+U8 = mybir.dt.uint8
+E4M3 = mybir.dt.float8_e4m3fn_x4
+E5M2 = mybir.dt.float8_e5m2_x4
+ALU = mybir.AluOpType
+ACT = mybir.ActivationFunctionType
+AX = mybir.AxisListType
+
+P = 128
+PACK = 4
+PASS = P * PACK
+PASSES = J // PASS
+BLOCKS = 2
+LIST_COLS = PASS // 16
+ABS_W = P + 8
+
+
+def tile_list_moment_products_sized_larger_kernel(tc, xf, ra, xb, gt, cb, old, offs, offs2, offs3, out):
+    nc = tc.nc
+    with ExitStack() as ctx:
+        keep = ctx.enter_context(tc.tile_pool(name="keep", bufs=1))
+        gbank = ctx.enter_context(tc.psum_pool(name="gbank", bufs=1))
+        ubank = ctx.enter_context(tc.psum_pool(name="ubank", bufs=2))
+        wbank = ctx.enter_context(tc.psum_pool(name="wbank", bufs=1))
+
+        def load_list(src, name):
+            t = keep.tile([P, J // 16], U16, name=name)
+            nc.sync.dma_start(t[:], src)
+            return t
+
+        def load_rows(src, b, name):
+            t = keep.tile([P, T], F32, name=name)
+            nc.sync.dma_start(t[:], src[b * P : (b + 1) * P, :])
+            return t
+
+        ident = keep.tile([P, P], F32, name="ident")
+        make_identity(nc, ident[:])
+
+        ra_sb = keep.tile([P, PASSES, PACK], F32, name="ra_sb")
+        cb_sb = keep.tile([P, PASSES, PACK], F32, name="cb_sb")
+        nc.scalar.dma_start(ra_sb[:], ra.rearrange("o (a p t) -> p a (t o)", a=PASSES, t=PACK))
+        list_g = load_list(offs3, "list_g")
+        g_tab = [load_rows(gt, b, "g_tab%d" % b) for b in range(BLOCKS)]
+        list_f = load_list(offs, "list_f")
+        nc.scalar.dma_start(cb_sb[:], cb.rearrange("(a p t) o -> p a (t o)", a=PASSES, t=PACK))
+        f_tab = [load_rows(xf, b, "f_tab%d" % b) for b in range(BLOCKS)]
+        list_b = load_list(offs2, "list_b")
+        b_tab = [load_rows(xb, b, "b_tab%d" % b) for b in range(BLOCKS)]
+        old_sb = keep.tile([P, BLOCKS, N], F32, name="old_sb")
+        nc.sync.dma_start(old_sb[:], old.rearrange("(b p) n -> p b n", p=P))
+
+        def picked(tab, lst, a):
+            return tab[:].indirect(lst[:, a * LIST_COLS : (a + 1) * LIST_COLS])
+
+        def gather(tab, lst, a, name, on_vector, times=None):
+            t = keep.tile([P, PASS], F32, name=name)
+            if times is not None:
+                nc.vector.tensor_tensor(t[:], picked(tab, lst, a), times, ALU.mult)
+            elif on_vector:
+                nc.vector.tensor_copy(t[:], picked(tab, lst, a))
+            else:
+                nc.scalar.activation(t[:], picked(tab, lst, a), ACT.Copy)
+            return t
+
+        ra_all = []
+        for a in range(PASSES):
+            bank = ubank.tile([P, PACK, P], F32, name="ra_bank%d" % a, tag="ubank")
+            for t in range(PACK):
+                nc.tensor.transpose(bank[:, t, :], ra_sb[:, a, t : t + 1].to_broadcast([P, P]), ident[:])
+            spread = keep.tile([P, PASS], F32, name="ra_all%d" % a)
+            nc.scalar.activation(spread[:].rearrange("p (q t) -> p q t", t=PACK), bank[:].rearrange("p t q -> p q t"), ACT.Copy)
+            ra_all.append(spread)
+        inv_cb = keep.tile([P, PASSES, PACK], F32, name="inv_cb")
+        nc.vector.reciprocal(inv_cb[:], cb_sb[:])
+
+        g_t = {}
+        g_abs = {}
+        for b in range(BLOCKS):
+            for a in range(PASSES):
+                g_abs[a, b] = keep.tile([P, PACK, ABS_W], F32, name="g_abs%d%d" % (a, b))
+        g_max = keep.tile([P, PASSES, PACK], F32, name="g_max")
+        for b in range(BLOCKS):
+            rows = [gather(g_tab[b], list_g, a, "g_rows%d%d" % (a, b), a == 0) for a in range(PASSES)]
+            for a in range(PASSES):
+                bank = gbank.tile([P, PACK, P], F32, name="g_t%d%d" % (a, b))
+                for t in range(PACK):
+                    nc.tensor.transpose(bank[:, t, :], rows[a][:, t:PASS:PACK], ident[:])
+                g_t[a, b] = bank
+                nc.scalar.activation(g_abs[a, b][:, :, 0:P], bank[:], ACT.Abs)
+                if b == 0:
+                    nc.vector.tensor_reduce(g_abs[a, 1][:, :, P], g_abs[a, 0][:, :, 0:P], AX.X, ALU.max)
+
+        f_rows = {}
+
+        def features(b, a, on_vector):
+            if on_vector:
+                f_rows[b, a] = gather(f_tab[b], list_f, a, "f_w%d%d" % (b, a), True, ra_all[a][:])
+            else:
+                plain = gather(f_tab[b], list_f, a, "f_rows%d%d" % (b, a), False)
+                weighted = keep.tile([P, PASS], F32, name="f_w%d%d" % (b, a))
+                nc.gpsimd.tensor_tensor(weighted[:], plain[:], ra_all[a][:], ALU.mult)
+                f_rows[b, a] = weighted
+
+        features(0, 0, True)
+        features(0, 1, False)
+
+        g_codes = []
+        g_scales = []
+        for a in range(PASSES):
+            den = keep.tile([P, PACK], F32, name="den%d" % a)
+            fac = keep.tile([P, PACK], F32, name="fac%d" % a)
+            nc.vector.tensor_reduce(g_max[:, a, :], g_abs[a, 1][:, :, 0 : P + 1], AX.X, ALU.max)
+            nc.vector.scalar_tensor_tensor(den[:], g_max[:, a, :], 0.2, inv_cb[:, a, :], ALU.add, ALU.mult)
+            nc.vector.reciprocal(fac[:], den[:])
+            g_bf = keep.tile([P, N, PACK], BF16, name="g_bf%d" % a, align_bytes=64)
+            for b in range(BLOCKS):
+                nc.vector.tensor_tensor(
+                    g_bf[:, b * P : (b + 1) * P, :],
+                    g_t[a, b][:].rearrange("p t n -> p n t"),
+                    fac[:].unsqueeze(1).to_broadcast([P, P, PACK]),
+                    ALU.mult,
+                )
+            codes = keep.tile([P, N], U32, name="g_codes%d" % a, align_bytes=64)
+            scales = keep.tile([P, N], U8, name="g_scales%d" % a, align_bytes=64)
+            nc.vector.quantize_mx(codes[:].bitcast(E5M2), scales[:], g_bf[:].rearrange("p n t -> p (n t)"))
+            g_codes.append(codes)
+            g_scales.append(scales)
+
+        features(1, 0, False)
+        features(1, 1, False)
+
+        old_s = keep.tile([P, BLOCKS, N], F32, name="old_s")
+        res = keep.tile([P, BLOCKS, N], F32, name="res")
+        for b in range(BLOCKS):
+            acc = wbank.tile([P, N], F32, name="acc%d" % b)
+            u_bf = []
+            for a in range(PASSES):
+                prod = keep.tile([P, PASS], BF16, name="prod%d%d" % (b, a))
+                if b == 1 and a == 0:
+                    full = gather(b_tab[b], list_b, a, "b_rows%d%d" % (b, a), True, f_rows[b, a][:])
+                    nc.vector.tensor_copy(prod[:], full[:])
+                else:
+                    rows_b = gather(b_tab[b], list_b, a, "b_rows%d%d" % (b, a), False)
+                    nc.vector.tensor_tensor(prod[:], rows_b[:], f_rows[b, a][:], ALU.mult)
+                u_bf.append(prod)
+            if b == 0:
+                nc.gpsimd.tensor_scalar(old_s[:], old_sb[:], 0.04, 0.0, ALU.mult, ALU.add)
+            for a in range(PASSES):
+                words = u_bf[a][:].bitcast(F32)
+                bank = ubank.tile([P, 2, P], F32, name="u_t%d%d" % (b, a), tag="ubank")
+                for u in range(2):
+                    nc.tensor.transpose(bank[:, u, :], words[:, u : 2 * P : 2], ident[:])
+                grouped = keep.tile([P, P * PACK], BF16, name="u_grp%d%d" % (b, a), align_bytes=64)
+                nc.scalar.copy(grouped[:].bitcast(F32).rearrange("p (k u) -> p k u", u=2), bank[:].rearrange("p u k -> p k u"))
+                codes = keep.tile([P, P], U32, name="u_codes%d%d" % (b, a), align_bytes=64)
+                scales = keep.tile([P, P], U8, name="u_scales%d%d" % (b, a), align_bytes=64)
+                nc.vector.quantize_mx(codes[:].bitcast(E4M3), scales[:], grouped[:])
+                nc.tensor.matmul_mx(
+                    acc[:],
+                    lhsT=codes[:].bitcast(E4M3),
+                    lhsT_scale=scales[:],
+                    rhs=g_codes[a][:].bitcast(E5M2),
+                    rhs_scale=g_scales[a][:],
+                    start=(a == 0),
+                    stop=(a == PASSES - 1),
+                )
+            nc.vector.scalar_tensor_tensor(res[:, b, :], acc[:], 0.04, old_s[:, b, :], ALU.mult, ALU.max)
+            nc.sync.dma_start(out[b * P : (b + 1) * P, :], res[:, b, :])

@@ -1,7 +1,6 @@
 from contextlib import ExitStack
 
 import concourse.mybir as mybir
-from concourse.masks import make_identity
 
 K, J, N, T = 256, 1024, 256, 2048
 FLOPS = 2 * K * J * N
@@ -18,6 +17,7 @@ ACT = mybir.ActivationFunctionType
 AX = mybir.AxisListType
 
 P = 128
+QUAD = 32
 PACK = 4
 PASS = P * PACK
 PASSES = J // PASS
@@ -30,9 +30,7 @@ def tile_list_moment_products_sized_larger_kernel(tc, xf, ra, xb, gt, cb, old, o
     nc = tc.nc
     with ExitStack() as ctx:
         keep = ctx.enter_context(tc.tile_pool(name="keep", bufs=1))
-        gbank = ctx.enter_context(tc.psum_pool(name="gbank", bufs=1))
-        ubank = ctx.enter_context(tc.psum_pool(name="ubank", bufs=2))
-        wbank = ctx.enter_context(tc.psum_pool(name="wbank", bufs=1))
+        psum = ctx.enter_context(tc.psum_pool(name="psum", bufs=1))
 
         def load_list(src, name):
             t = keep.tile([P, J // 16], U16, name=name)
@@ -40,42 +38,54 @@ def tile_list_moment_products_sized_larger_kernel(tc, xf, ra, xb, gt, cb, old, o
             return t
 
         def load_rows(src, b, name):
-            t = keep.tile([P, T], F32, name=name)
+            t = keep.tile([P, T], F32, name=name, align_bytes=64)
             nc.sync.dma_start(t[:], src[b * P : (b + 1) * P, :])
             return t
 
-        ident = keep.tile([P, P], F32, name="ident")
-        make_identity(nc, ident[:])
-
         ra_sb = keep.tile([P, PASSES, PACK], F32, name="ra_sb")
         cb_sb = keep.tile([P, PASSES, PACK], F32, name="cb_sb")
-        nc.scalar.dma_start(ra_sb[:], ra.rearrange("o (a p t) -> p a (t o)", a=PASSES, t=PACK))
+        nc.sync.dma_start(ra_sb[:], ra.rearrange("o (a p t) -> p a (t o)", a=PASSES, t=PACK))
+        g_tab = [load_rows(gt, 0, "g_tab0")]
         list_g = load_list(offs3, "list_g")
-        g_tab = [load_rows(gt, b, "g_tab%d" % b) for b in range(BLOCKS)]
+        nc.sync.dma_start(cb_sb[:], cb.rearrange("(a p t) o -> p a (t o)", a=PASSES, t=PACK))
+        g_tab.append(load_rows(gt, 1, "g_tab1"))
         list_f = load_list(offs, "list_f")
-        nc.scalar.dma_start(cb_sb[:], cb.rearrange("(a p t) o -> p a (t o)", a=PASSES, t=PACK))
         f_tab = [load_rows(xf, b, "f_tab%d" % b) for b in range(BLOCKS)]
         list_b = load_list(offs2, "list_b")
         b_tab = [load_rows(xb, b, "b_tab%d" % b) for b in range(BLOCKS)]
         old_sb = keep.tile([P, BLOCKS, N], F32, name="old_sb")
         nc.sync.dma_start(old_sb[:], old.rearrange("(b p) n -> p b n", p=P))
 
+        ident = keep.tile([P, P], F32, name="ident")
+        ones = keep.tile([P, P], F32, name="ones")
+        col = keep.tile([P, P], F32, name="col", align_bytes=64)
+        row = keep.tile([P, P], F32, name="row", align_bytes=64)
+        nc.vector.memset(ones[:], 1.0)
+        nc.vector.memset(ident[:], 0.0)
+        nc.vector.tensor_tensor_scan(col[:], ones[:], ones[:], 0.0, ALU.mult, ALU.add)
+        nc.vector.transpose(row[:], col[:])
+        for q in range(P // QUAD):
+            s = slice(QUAD * q, QUAD * (q + 1))
+            nc.vector.tensor_tensor(ident[s, s], row[s, s], col[s, s], ALU.is_equal)
+        warm = keep.tile([P, 1], F32, name="warm")
+        nc.scalar.activation(warm[:], ones[:, 0:1], ACT.Abs)
+
         def picked(tab, lst, a):
             return tab[:].indirect(lst[:, a * LIST_COLS : (a + 1) * LIST_COLS])
 
-        def gather(tab, lst, a, name, on_vector, times=None):
+        def gather_vector(tab, lst, a, name):
             t = keep.tile([P, PASS], F32, name=name)
-            if times is not None:
-                nc.vector.tensor_tensor(t[:], picked(tab, lst, a), times, ALU.mult)
-            elif on_vector:
-                nc.vector.tensor_copy(t[:], picked(tab, lst, a))
-            else:
-                nc.scalar.activation(t[:], picked(tab, lst, a), ACT.Copy)
+            nc.vector.tensor_copy(t[:], picked(tab, lst, a))
+            return t
+
+        def gather_scalar(tab, lst, a, name):
+            t = keep.tile([P, PASS], F32, name=name)
+            nc.scalar.activation(t[:], picked(tab, lst, a), ACT.Copy)
             return t
 
         ra_all = []
         for a in range(PASSES):
-            bank = ubank.tile([P, PACK, P], F32, name="ra_bank%d" % a, tag="ubank")
+            bank = psum.tile([P, PACK, P], F32, name="ra_bank%d" % a, tag="spare%d" % a)
             for t in range(PACK):
                 nc.tensor.transpose(bank[:, t, :], ra_sb[:, a, t : t + 1].to_broadcast([P, P]), ident[:])
             spread = keep.tile([P, PASS], F32, name="ra_all%d" % a)
@@ -85,95 +95,97 @@ def tile_list_moment_products_sized_larger_kernel(tc, xf, ra, xb, gt, cb, old, o
         nc.vector.reciprocal(inv_cb[:], cb_sb[:])
 
         g_t = {}
-        g_abs = {}
         for b in range(BLOCKS):
+            rows = [gather_vector(g_tab[b], list_g, 0, "g_rows0%d" % b), gather_scalar(g_tab[b], list_g, 1, "g_rows1%d" % b)]
             for a in range(PASSES):
-                g_abs[a, b] = keep.tile([P, PACK, ABS_W], F32, name="g_abs%d%d" % (a, b))
-        g_max = keep.tile([P, PASSES, PACK], F32, name="g_max")
-        for b in range(BLOCKS):
-            rows = [gather(g_tab[b], list_g, a, "g_rows%d%d" % (a, b), a == 0) for a in range(PASSES)]
-            for a in range(PASSES):
-                bank = gbank.tile([P, PACK, P], F32, name="g_t%d%d" % (a, b))
+                bank = psum.tile([P, PACK, P], F32, name="g_t%d%d" % (a, b))
                 for t in range(PACK):
                     nc.tensor.transpose(bank[:, t, :], rows[a][:, t:PASS:PACK], ident[:])
                 g_t[a, b] = bank
-                nc.scalar.activation(g_abs[a, b][:, :, 0:P], bank[:], ACT.Abs)
-                if b == 0:
-                    nc.vector.tensor_reduce(g_abs[a, 1][:, :, P], g_abs[a, 0][:, :, 0:P], AX.X, ALU.max)
 
-        f_rows = {}
+        abs_lo = keep.tile([P, PASSES, PACK, P], F32, name="abs_lo", tag="g_tab1", align_bytes=64)
+        abs_hi = [keep.tile([P, PACK, ABS_W], F32, name="abs_hi%d" % a) for a in range(PASSES)]
+        for a in range(PASSES):
+            nc.scalar.activation(abs_lo[:, a], g_t[a, 0][:], ACT.Abs)
+            nc.vector.tensor_reduce(abs_hi[a][:, :, P], abs_lo[:, a], AX.X, ALU.max)
 
-        def features(b, a, on_vector):
-            if on_vector:
-                f_rows[b, a] = gather(f_tab[b], list_f, a, "f_w%d%d" % (b, a), True, ra_all[a][:])
-            else:
-                plain = gather(f_tab[b], list_f, a, "f_rows%d%d" % (b, a), False)
-                weighted = keep.tile([P, PASS], F32, name="f_w%d%d" % (b, a))
-                nc.gpsimd.tensor_tensor(weighted[:], plain[:], ra_all[a][:], ALU.mult)
-                f_rows[b, a] = weighted
+        f_w = {}
+        for a in range(PASSES):
+            f_w[0, a] = keep.tile([P, PASS], F32, name="f_w0%d" % a)
+            nc.vector.tensor_tensor(f_w[0, a][:], picked(f_tab[0], list_f, a), ra_all[a][:], ALU.mult)
 
-        features(0, 0, True)
-        features(0, 1, False)
+        fac = []
+        for a in range(PASSES):
+            g_max = keep.tile([P, PACK], F32, name="g_max%d" % a)
+            den = keep.tile([P, PACK], F32, name="den%d" % a)
+            fac.append(keep.tile([P, PACK], F32, name="fac%d" % a))
+            nc.scalar.activation(abs_hi[a][:, :, 0:P], g_t[a, 1][:], ACT.Abs)
+            nc.vector.tensor_reduce(g_max[:], abs_hi[a][:, :, 0 : P + 1], AX.X, ALU.max)
+            nc.vector.scalar_tensor_tensor(den[:], g_max[:], 0.2, inv_cb[:, a, :], ALU.add, ALU.mult)
+            nc.vector.reciprocal(fac[a][:], den[:])
+
+        g_bf = []
+        for a in range(PASSES):
+            g_bf.append(keep.tile([P, N, PACK], BF16, name="g_bf%d" % a, align_bytes=64))
+            for b in range(BLOCKS):
+                nc.vector.tensor_tensor(
+                    g_bf[a][:, b * P : (b + 1) * P, :],
+                    g_t[a, b][:].rearrange("p t n -> p n t"),
+                    fac[a][:].unsqueeze(1).to_broadcast([P, P, PACK]),
+                    ALU.mult,
+                )
+
+        for a in range(PASSES):
+            plain = gather_scalar(f_tab[1], list_f, a, "f_rows%d" % a)
+            f_w[1, a] = keep.tile([P, PASS], F32, name="f_w1%d" % a)
+            nc.gpsimd.tensor_tensor(f_w[1, a][:], plain[:], ra_all[a][:], ALU.mult)
 
         g_codes = []
         g_scales = []
         for a in range(PASSES):
-            den = keep.tile([P, PACK], F32, name="den%d" % a)
-            fac = keep.tile([P, PACK], F32, name="fac%d" % a)
-            nc.vector.tensor_reduce(g_max[:, a, :], g_abs[a, 1][:, :, 0 : P + 1], AX.X, ALU.max)
-            nc.vector.scalar_tensor_tensor(den[:], g_max[:, a, :], 0.2, inv_cb[:, a, :], ALU.add, ALU.mult)
-            nc.vector.reciprocal(fac[:], den[:])
-            g_bf = keep.tile([P, N, PACK], BF16, name="g_bf%d" % a, align_bytes=64)
-            for b in range(BLOCKS):
-                nc.vector.tensor_tensor(
-                    g_bf[:, b * P : (b + 1) * P, :],
-                    g_t[a, b][:].rearrange("p t n -> p n t"),
-                    fac[:].unsqueeze(1).to_broadcast([P, P, PACK]),
-                    ALU.mult,
-                )
-            codes = keep.tile([P, N], U32, name="g_codes%d" % a, align_bytes=64)
-            scales = keep.tile([P, N], U8, name="g_scales%d" % a, align_bytes=64)
-            nc.vector.quantize_mx(codes[:].bitcast(E5M2), scales[:], g_bf[:].rearrange("p n t -> p (n t)"))
-            g_codes.append(codes)
-            g_scales.append(scales)
+            g_codes.append(keep.tile([P, N], U32, name="g_codes%d" % a, align_bytes=64))
+            g_scales.append(keep.tile([P, N], U8, name="g_scales%d" % a, align_bytes=64))
+            nc.vector.quantize_mx(g_codes[a][:].bitcast(E5M2), g_scales[a][:], g_bf[a][:].rearrange("p n t -> p (n t)"))
 
-        features(1, 0, False)
-        features(1, 1, False)
+        prod = {}
+        for b in range(BLOCKS):
+            for a in range(PASSES):
+                rows_b = gather_scalar(b_tab[b], list_b, a, "b_rows%d%d" % (b, a))
+                prod[b, a] = keep.tile([P, PASS], BF16, name="prod%d%d" % (b, a))
+                engine = nc.gpsimd if (b, a) == (0, 0) else nc.vector
+                engine.tensor_tensor(prod[b, a][:], rows_b[:], f_w[b, a][:], ALU.mult)
 
         old_s = keep.tile([P, BLOCKS, N], F32, name="old_s")
-        res = keep.tile([P, BLOCKS, N], F32, name="res")
+        nc.gpsimd.tensor_scalar(old_s[:], old_sb[:], 0.04, 0.0, ALU.mult, ALU.add)
+
+        grouped_lo = keep.tile([P, PASSES, PASS], BF16, name="grouped_lo", tag="b_tab1", align_bytes=64)
+        grouped_hi = keep.tile([P, PASSES, PASS], BF16, name="grouped_hi", align_bytes=64)
+        u_codes = {}
+        u_scales = {}
         for b in range(BLOCKS):
-            acc = wbank.tile([P, N], F32, name="acc%d" % b)
-            u_bf = []
             for a in range(PASSES):
-                prod = keep.tile([P, PASS], BF16, name="prod%d%d" % (b, a))
-                if b == 1 and a == 0:
-                    full = gather(b_tab[b], list_b, a, "b_rows%d%d" % (b, a), True, f_rows[b, a][:])
-                    nc.vector.tensor_copy(prod[:], full[:])
-                else:
-                    rows_b = gather(b_tab[b], list_b, a, "b_rows%d%d" % (b, a), False)
-                    nc.vector.tensor_tensor(prod[:], rows_b[:], f_rows[b, a][:], ALU.mult)
-                u_bf.append(prod)
-            if b == 0:
-                nc.gpsimd.tensor_scalar(old_s[:], old_sb[:], 0.04, 0.0, ALU.mult, ALU.add)
-            for a in range(PASSES):
-                words = u_bf[a][:].bitcast(F32)
-                bank = ubank.tile([P, 2, P], F32, name="u_t%d%d" % (b, a), tag="ubank")
+                words = prod[b, a][:].bitcast(F32)
+                bank = psum.tile([P, 2, P], F32, name="u_t%d%d" % (b, a), tag=("spare%d" % a) if b == 0 else ("g_t%d0" % a))
                 for u in range(2):
                     nc.tensor.transpose(bank[:, u, :], words[:, u : 2 * P : 2], ident[:])
-                grouped = keep.tile([P, P * PACK], BF16, name="u_grp%d%d" % (b, a), align_bytes=64)
-                nc.scalar.copy(grouped[:].bitcast(F32).rearrange("p (k u) -> p k u", u=2), bank[:].rearrange("p u k -> p k u"))
-                codes = keep.tile([P, P], U32, name="u_codes%d%d" % (b, a), align_bytes=64)
-                scales = keep.tile([P, P], U8, name="u_scales%d%d" % (b, a), align_bytes=64)
-                nc.vector.quantize_mx(codes[:].bitcast(E4M3), scales[:], grouped[:])
+                grouped = (grouped_lo, grouped_hi)[b][:, a, :]
+                nc.scalar.copy(grouped.bitcast(F32).rearrange("p (k u) -> p k u", u=2), bank[:].rearrange("p u k -> p k u"))
+                u_codes[b, a] = keep.tile([P, P], U32, name="u_codes%d%d" % (b, a), align_bytes=64)
+                u_scales[b, a] = keep.tile([P, P], U8, name="u_scales%d%d" % (b, a), align_bytes=64)
+                nc.vector.quantize_mx(u_codes[b, a][:].bitcast(E4M3), u_scales[b, a][:], grouped)
+
+        for b in range(BLOCKS):
+            acc = psum.tile([P, N], F32, name="acc%d" % b)
+            for a in range(PASSES):
                 nc.tensor.matmul_mx(
                     acc[:],
-                    lhsT=codes[:].bitcast(E4M3),
-                    lhsT_scale=scales[:],
+                    lhsT=u_codes[b, a][:].bitcast(E4M3),
+                    lhsT_scale=u_scales[b, a][:],
                     rhs=g_codes[a][:].bitcast(E5M2),
                     rhs_scale=g_scales[a][:],
                     start=(a == 0),
                     stop=(a == PASSES - 1),
                 )
-            nc.vector.scalar_tensor_tensor(res[:, b, :], acc[:], 0.04, old_s[:, b, :], ALU.mult, ALU.max)
-            nc.sync.dma_start(out[b * P : (b + 1) * P, :], res[:, b, :])
+            res = keep.tile([P, N], F32, name="res%d" % b)
+            nc.vector.scalar_tensor_tensor(res[:], acc[:], 0.04, old_s[:, b, :], ALU.mult, ALU.max)
+            nc.sync.dma_start(out[b * P : (b + 1) * P, :], res[:])

@@ -42,15 +42,16 @@ def tile_list_moment_products_sized_larger_kernel(tc, xf, ra, xb, gt, cb, old, o
             nc.sync.dma_start(t[:], src[b * P : (b + 1) * P, :])
             return t
 
-        ra_sb = keep.tile([P, PASSES, PACK], F32, name="ra_sb")
+        ra_sb = keep.tile([P, J // P], F32, name="ra_sb")
         cb_sb = keep.tile([P, PASSES, PACK], F32, name="cb_sb")
-        nc.sync.dma_start(ra_sb[:], ra.rearrange("o (a p t) -> p a (t o)", a=PASSES, t=PACK))
+        nc.sync.dma_start(ra_sb[:], ra.rearrange("o (p c) -> (o p) c", p=P))
         g_tab = [load_rows(gt, 0, "g_tab0")]
         list_g = load_list(offs3, "list_g")
-        nc.sync.dma_start(cb_sb[:], cb.rearrange("(a p t) o -> p a (t o)", a=PASSES, t=PACK))
         g_tab.append(load_rows(gt, 1, "g_tab1"))
         list_f = load_list(offs, "list_f")
-        f_tab = [load_rows(xf, b, "f_tab%d" % b) for b in range(BLOCKS)]
+        f_tab = [load_rows(xf, 0, "f_tab0")]
+        nc.sync.dma_start(cb_sb[:], cb.rearrange("(a p t) o -> p a (t o)", a=PASSES, t=PACK))
+        f_tab.append(load_rows(xf, 1, "f_tab1"))
         list_b = load_list(offs2, "list_b")
         b_tab = [load_rows(xb, b, "b_tab%d" % b) for b in range(BLOCKS)]
         old_sb = keep.tile([P, BLOCKS, N], F32, name="old_sb")
@@ -83,14 +84,18 @@ def tile_list_moment_products_sized_larger_kernel(tc, xf, ra, xb, gt, cb, old, o
             nc.scalar.activation(t[:], picked(tab, lst, a), ACT.Copy)
             return t
 
-        ra_all = []
-        for a in range(PASSES):
-            bank = psum.tile([P, PACK, P], F32, name="ra_bank%d" % a, tag="spare%d" % a)
-            for t in range(PACK):
-                nc.tensor.transpose(bank[:, t, :], ra_sb[:, a, t : t + 1].to_broadcast([P, P]), ident[:])
-            spread = keep.tile([P, PASS], F32, name="ra_all%d" % a)
-            nc.scalar.activation(spread[:].rearrange("p (q t) -> p q t", t=PACK), bank[:].rearrange("p t q -> p q t"), ACT.Copy)
-            ra_all.append(spread)
+        ra_spread = keep.tile([P, J], F32, name="ra_spread")
+        for h in range(2):
+            bank = psum.tile([P, PACK, P], F32, name="ra_bank%d" % h, tag="spare%d" % h)
+            for c in range(PACK):
+                column = ra_sb[:, PACK * h + c : PACK * h + c + 1]
+                nc.tensor.transpose(bank[:, c, :], column.to_broadcast([P, P]), ident[:])
+            nc.scalar.activation(
+                ra_spread[:].rearrange("p (q h c) -> p h q c", h=2, c=PACK)[:, h],
+                bank[:].rearrange("p c q -> p q c"),
+                ACT.Copy,
+            )
+        ra_all = [ra_spread[:, a * PASS : (a + 1) * PASS] for a in range(PASSES)]
         inv_cb = keep.tile([P, PASSES, PACK], F32, name="inv_cb")
         nc.vector.reciprocal(inv_cb[:], cb_sb[:])
 
@@ -112,7 +117,7 @@ def tile_list_moment_products_sized_larger_kernel(tc, xf, ra, xb, gt, cb, old, o
         f_w = {}
         for a in range(PASSES):
             f_w[0, a] = keep.tile([P, PASS], F32, name="f_w0%d" % a)
-            nc.vector.tensor_tensor(f_w[0, a][:], picked(f_tab[0], list_f, a), ra_all[a][:], ALU.mult)
+            nc.vector.tensor_tensor(f_w[0, a][:], picked(f_tab[0], list_f, a), ra_all[a], ALU.mult)
 
         fac = []
         for a in range(PASSES):
@@ -137,8 +142,8 @@ def tile_list_moment_products_sized_larger_kernel(tc, xf, ra, xb, gt, cb, old, o
 
         for a in range(PASSES):
             plain = gather_scalar(f_tab[1], list_f, a, "f_rows%d" % a)
-            f_w[1, a] = keep.tile([P, PASS], F32, name="f_w1%d" % a)
-            nc.gpsimd.tensor_tensor(f_w[1, a][:], plain[:], ra_all[a][:], ALU.mult)
+            f_w[1, a] = keep.tile([P, PASS], F32, name="f_w1%d" % a, tag=("f_w10", "g_max1")[a])
+            nc.gpsimd.tensor_tensor(f_w[1, a][:], plain[:], ra_all[a], ALU.mult)
 
         g_codes = []
         g_scales = []
@@ -156,7 +161,7 @@ def tile_list_moment_products_sized_larger_kernel(tc, xf, ra, xb, gt, cb, old, o
                 engine.tensor_tensor(prod[b, a][:], rows_b[:], f_w[b, a][:], ALU.mult)
 
         old_s = keep.tile([P, BLOCKS, N], F32, name="old_s")
-        nc.gpsimd.tensor_scalar(old_s[:], old_sb[:], 0.04, 0.0, ALU.mult, ALU.add)
+        nc.scalar.activation(old_s[:], old_sb[:], ACT.Copy, scale=0.04)
 
         grouped_lo = keep.tile([P, PASSES, PASS], BF16, name="grouped_lo", tag="b_tab1", align_bytes=64)
         grouped_hi = keep.tile([P, PASSES, PASS], BF16, name="grouped_hi", align_bytes=64)

@@ -23,7 +23,6 @@ PASS = P * PACK
 PASSES = J // PASS
 BLOCKS = 2
 LIST_COLS = PASS // 16
-ABS_W = P + 8
 
 
 def tile_list_moment_products_sized_larger_kernel(tc, xf, ra, xb, gt, cb, old, offs, offs2, offs3, out):
@@ -80,7 +79,7 @@ def tile_list_moment_products_sized_larger_kernel(tc, xf, ra, xb, gt, cb, old, o
             return t
 
         def gather_scalar(tab, lst, a, name):
-            t = keep.tile([P, PASS], F32, name=name)
+            t = keep.tile([P, PASS], F32, name=name, align_bytes=64)
             nc.scalar.activation(t[:], picked(tab, lst, a), ACT.Copy)
             return t
 
@@ -96,8 +95,6 @@ def tile_list_moment_products_sized_larger_kernel(tc, xf, ra, xb, gt, cb, old, o
                 ACT.Copy,
             )
         ra_all = [ra_spread[:, a * PASS : (a + 1) * PASS] for a in range(PASSES)]
-        inv_cb = keep.tile([P, PASSES, PACK], F32, name="inv_cb")
-        nc.vector.reciprocal(inv_cb[:], cb_sb[:])
 
         g_t = {}
         for b in range(BLOCKS):
@@ -108,26 +105,29 @@ def tile_list_moment_products_sized_larger_kernel(tc, xf, ra, xb, gt, cb, old, o
                     nc.tensor.transpose(bank[:, t, :], rows[a][:, t:PASS:PACK], ident[:])
                 g_t[a, b] = bank
 
-        abs_lo = keep.tile([P, PASSES, PACK, P], F32, name="abs_lo", tag="g_tab1", align_bytes=64)
-        abs_hi = [keep.tile([P, PACK, ABS_W], F32, name="abs_hi%d" % a) for a in range(PASSES)]
-        for a in range(PASSES):
-            nc.scalar.activation(abs_lo[:, a], g_t[a, 0][:], ACT.Abs)
-            nc.vector.tensor_reduce(abs_hi[a][:, :, P], abs_lo[:, a], AX.X, ALU.max)
+        g_abs = keep.tile([P, PASSES, PACK, N], F32, name="g_abs", tag="g_tab1", align_bytes=64)
+        for b in range(BLOCKS):
+            for a in range(PASSES):
+                nc.scalar.activation(g_abs[:, a, :, b * P : (b + 1) * P], g_t[a, b][:], ACT.Abs)
 
         f_w = {}
+        f_first = keep.tile([P, J], F32, name="f_first")
+        nc.vector.tensor_tensor(f_first[:], f_tab[0][:].indirect(list_f[:]), ra_spread[:], ALU.mult)
         for a in range(PASSES):
-            f_w[0, a] = keep.tile([P, PASS], F32, name="f_w0%d" % a)
-            nc.vector.tensor_tensor(f_w[0, a][:], picked(f_tab[0], list_f, a), ra_all[a], ALU.mult)
+            f_w[0, a] = f_first[:, a * PASS : (a + 1) * PASS]
 
+        max_pair = keep.tile([P, PASSES, PACK, 2], F32, name="max_pair", tag="f_tab0", align_bytes=64)
+        inv_pair = keep.tile([P, PASSES, PACK, 2], F32, name="inv_pair")
+        nc.vector.tensor_scalar(max_pair[:, :, :, 1], ones[:, 0 : PASSES * PACK].rearrange("p (a t) -> p a t", t=PACK), 0.2, None, ALU.mult)
+        nc.vector.tensor_copy(inv_pair[:, :, :, 1], cb_sb[:])
         fac = []
         for a in range(PASSES):
-            g_max = keep.tile([P, PACK], F32, name="g_max%d" % a)
             den = keep.tile([P, PACK], F32, name="den%d" % a)
             fac.append(keep.tile([P, PACK], F32, name="fac%d" % a))
-            nc.scalar.activation(abs_hi[a][:, :, 0:P], g_t[a, 1][:], ACT.Abs)
-            nc.vector.tensor_reduce(g_max[:], abs_hi[a][:, :, 0 : P + 1], AX.X, ALU.max)
-            nc.vector.scalar_tensor_tensor(den[:], g_max[:], 0.2, inv_cb[:, a, :], ALU.add, ALU.mult)
-            nc.vector.reciprocal(fac[a][:], den[:])
+            nc.vector.tensor_reduce(max_pair[:, a, :, 0], g_abs[:, a], AX.X, ALU.max)
+            nc.vector.tensor_reduce(den[:], max_pair[:, a], AX.X, ALU.add)
+            nc.vector.reciprocal(inv_pair[:, a, :, 0], den[:])
+            nc.vector.tensor_reduce(fac[a][:], inv_pair[:, a], AX.X, ALU.mult)
 
         g_bf = []
         for a in range(PASSES):
@@ -142,15 +142,19 @@ def tile_list_moment_products_sized_larger_kernel(tc, xf, ra, xb, gt, cb, old, o
 
         for a in range(PASSES):
             plain = gather_scalar(f_tab[1], list_f, a, "f_rows%d" % a)
-            f_w[1, a] = keep.tile([P, PASS], F32, name="f_w1%d" % a, tag=("f_w10", "g_max1")[a])
-            nc.gpsimd.tensor_tensor(f_w[1, a][:], plain[:], ra_all[a], ALU.mult)
+            weighted = keep.tile([P, PASS], F32, name="f_w1%d" % a)
+            nc.gpsimd.tensor_tensor(weighted[:], plain[:], ra_all[a], ALU.mult)
+            f_w[1, a] = weighted[:]
 
         g_codes = []
         g_scales = []
-        for a in range(PASSES):
-            g_codes.append(keep.tile([P, N], U32, name="g_codes%d" % a, align_bytes=64))
+
+        def quantize_gradients(a, slot):
+            g_codes.append(keep.tile([P, N], U32, name="g_codes%d" % a, tag=slot, align_bytes=64))
             g_scales.append(keep.tile([P, N], U8, name="g_scales%d" % a, align_bytes=64))
             nc.vector.quantize_mx(g_codes[a][:].bitcast(E5M2), g_scales[a][:], g_bf[a][:].rearrange("p n t -> p (n t)"))
+
+        quantize_gradients(0, "g_codes0")
 
         prod = {}
         for b in range(BLOCKS):
@@ -158,10 +162,12 @@ def tile_list_moment_products_sized_larger_kernel(tc, xf, ra, xb, gt, cb, old, o
                 rows_b = gather_scalar(b_tab[b], list_b, a, "b_rows%d%d" % (b, a))
                 prod[b, a] = keep.tile([P, PASS], BF16, name="prod%d%d" % (b, a))
                 engine = nc.gpsimd if (b, a) == (0, 0) else nc.vector
-                engine.tensor_tensor(prod[b, a][:], rows_b[:], f_w[b, a][:], ALU.mult)
+                engine.tensor_tensor(prod[b, a][:], rows_b[:], f_w[b, a], ALU.mult)
 
-        old_s = keep.tile([P, BLOCKS, N], F32, name="old_s")
-        nc.scalar.activation(old_s[:], old_sb[:], ACT.Copy, scale=0.04)
+        quantize_gradients(1, "b_rows10")
+
+        old_s = keep.tile([P, BLOCKS, N], F32, name="old_s", tag="b_rows11", align_bytes=64)
+        nc.vector.tensor_scalar(old_s[:], old_sb[:], 0.04, None, ALU.mult)
 
         grouped_lo = keep.tile([P, PASSES, PASS], BF16, name="grouped_lo", tag="b_tab1", align_bytes=64)
         grouped_hi = keep.tile([P, PASSES, PASS], BF16, name="grouped_hi", align_bytes=64)

@@ -23,6 +23,7 @@ PASS = P * PACK
 PASSES = J // PASS
 BLOCKS = 2
 LIST_COLS = PASS // 16
+LAST = (BLOCKS - 1, PASSES - 1)
 
 
 def tile_list_moment_products_sized_larger_kernel(tc, xf, ra, xb, gt, cb, old, offs, offs2, offs3, out):
@@ -42,15 +43,14 @@ def tile_list_moment_products_sized_larger_kernel(tc, xf, ra, xb, gt, cb, old, o
             return t
 
         ra_sb = keep.tile([P, J // P], F32, name="ra_sb")
-        cb_sb = keep.tile([P, PASSES, PACK], F32, name="cb_sb")
+        inv_pair = keep.tile([P, 2, PASSES, PACK], F32, name="inv_pair")
         nc.sync.dma_start(ra_sb[:], ra.rearrange("o (p c) -> (o p) c", p=P))
         g_tab = [load_rows(gt, 0, "g_tab0")]
         list_g = load_list(offs3, "list_g")
         g_tab.append(load_rows(gt, 1, "g_tab1"))
         list_f = load_list(offs, "list_f")
-        f_tab = [load_rows(xf, 0, "f_tab0")]
-        nc.sync.dma_start(cb_sb[:], cb.rearrange("(a p t) o -> p a (t o)", a=PASSES, t=PACK))
-        f_tab.append(load_rows(xf, 1, "f_tab1"))
+        f_tab = [load_rows(xf, b, "f_tab%d" % b) for b in range(BLOCKS)]
+        nc.sync.dma_start(inv_pair[:, 1], cb.rearrange("(a p t) o -> p a (t o)", a=PASSES, t=PACK))
         list_b = load_list(offs2, "list_b")
         b_tab = [load_rows(xb, b, "b_tab%d" % b) for b in range(BLOCKS)]
         old_sb = keep.tile([P, BLOCKS, N], F32, name="old_sb")
@@ -117,17 +117,15 @@ def tile_list_moment_products_sized_larger_kernel(tc, xf, ra, xb, gt, cb, old, o
             f_w[0, a] = f_first[:, a * PASS : (a + 1) * PASS]
 
         max_pair = keep.tile([P, PASSES, PACK, 2], F32, name="max_pair", tag="f_tab0", align_bytes=64)
-        inv_pair = keep.tile([P, PASSES, PACK, 2], F32, name="inv_pair")
         nc.vector.tensor_scalar(max_pair[:, :, :, 1], ones[:, 0 : PASSES * PACK].rearrange("p (a t) -> p a t", t=PACK), 0.2, None, ALU.mult)
-        nc.vector.tensor_copy(inv_pair[:, :, :, 1], cb_sb[:])
         fac = []
         for a in range(PASSES):
             den = keep.tile([P, PACK], F32, name="den%d" % a)
             fac.append(keep.tile([P, PACK], F32, name="fac%d" % a))
             nc.vector.tensor_reduce(max_pair[:, a, :, 0], g_abs[:, a], AX.X, ALU.max)
             nc.vector.tensor_reduce(den[:], max_pair[:, a], AX.X, ALU.add)
-            nc.vector.reciprocal(inv_pair[:, a, :, 0], den[:])
-            nc.vector.tensor_reduce(fac[a][:], inv_pair[:, a], AX.X, ALU.mult)
+            nc.vector.reciprocal(inv_pair[:, 0, a], den[:])
+            nc.vector.tensor_reduce(fac[a][:], inv_pair[:, :, a].rearrange("p s t -> p t s"), AX.X, ALU.mult)
 
         g_bf = []
         for a in range(PASSES):
@@ -159,14 +157,20 @@ def tile_list_moment_products_sized_larger_kernel(tc, xf, ra, xb, gt, cb, old, o
         prod = {}
         for b in range(BLOCKS):
             for a in range(PASSES):
-                rows_b = gather_scalar(b_tab[b], list_b, a, "b_rows%d%d" % (b, a))
                 prod[b, a] = keep.tile([P, PASS], BF16, name="prod%d%d" % (b, a))
                 engine = nc.gpsimd if (b, a) == (0, 0) else nc.vector
-                engine.tensor_tensor(prod[b, a][:], rows_b[:], f_w[b, a], ALU.mult)
+                parts = 2 if (b, a) == LAST else 1
+                width = PASS // parts
+                for h in range(parts):
+                    rows_b = keep.tile([P, width], F32, name="b_rows%d%d%d" % (b, a, h), align_bytes=64)
+                    first = (a * PASS + h * width) // 16
+                    nc.scalar.activation(rows_b[:], b_tab[b][:].indirect(list_b[:, first : first + width // 16]), ACT.Copy)
+                    cols = slice(h * width, (h + 1) * width)
+                    engine.tensor_tensor(prod[b, a][:, cols], rows_b[:], f_w[b, a][:, cols], ALU.mult)
 
-        quantize_gradients(1, "b_rows10")
+        quantize_gradients(1, "b_rows100")
 
-        old_s = keep.tile([P, BLOCKS, N], F32, name="old_s", tag="b_rows11", align_bytes=64)
+        old_s = keep.tile([P, BLOCKS, N], F32, name="old_s", tag="b_rows111", align_bytes=64)
         nc.vector.tensor_scalar(old_s[:], old_sb[:], 0.04, None, ALU.mult)
 
         grouped_lo = keep.tile([P, PASSES, PASS], BF16, name="grouped_lo", tag="b_tab1", align_bytes=64)
@@ -179,24 +183,34 @@ def tile_list_moment_products_sized_larger_kernel(tc, xf, ra, xb, gt, cb, old, o
                 bank = psum.tile([P, 2, P], F32, name="u_t%d%d" % (b, a), tag=("spare%d" % a) if b == 0 else ("g_t%d0" % a))
                 for u in range(2):
                     nc.tensor.transpose(bank[:, u, :], words[:, u : 2 * P : 2], ident[:])
-                grouped = (grouped_lo, grouped_hi)[b][:, a, :]
-                nc.scalar.copy(grouped.bitcast(F32).rearrange("p (k u) -> p k u", u=2), bank[:].rearrange("p u k -> p k u"))
                 u_codes[b, a] = keep.tile([P, P], U32, name="u_codes%d%d" % (b, a), align_bytes=64)
                 u_scales[b, a] = keep.tile([P, P], U8, name="u_scales%d%d" % (b, a), align_bytes=64)
-                nc.vector.quantize_mx(u_codes[b, a][:].bitcast(E4M3), u_scales[b, a][:], grouped)
+                parts = 2 if (b, a) == LAST else 1
+                width = P // parts
+                for h in range(parts):
+                    cols = slice(h * width, (h + 1) * width)
+                    grouped = (grouped_lo, grouped_hi)[b][:, a, PACK * h * width : PACK * (h + 1) * width]
+                    nc.scalar.copy(grouped.bitcast(F32).rearrange("p (k u) -> p k u", u=2), bank[:, :, cols].rearrange("p u k -> p k u"))
+                    nc.vector.quantize_mx(u_codes[b, a][:, cols].bitcast(E4M3), u_scales[b, a][:, cols], grouped)
 
         for b in range(BLOCKS):
-            acc = psum.tile([P, N], F32, name="acc%d" % b)
+            parts = 2 if b == BLOCKS - 1 else 1
+            width = N // parts
+            accs = [psum.tile([P, width], F32, name="acc%d%d" % (b, h), tag=("acc%d" % b, "g_t01")[h]) for h in range(parts)]
             for a in range(PASSES):
-                nc.tensor.matmul_mx(
-                    acc[:],
-                    lhsT=u_codes[b, a][:].bitcast(E4M3),
-                    lhsT_scale=u_scales[b, a][:],
-                    rhs=g_codes[a][:].bitcast(E5M2),
-                    rhs_scale=g_scales[a][:],
-                    start=(a == 0),
-                    stop=(a == PASSES - 1),
-                )
-            res = keep.tile([P, N], F32, name="res%d" % b)
-            nc.vector.scalar_tensor_tensor(res[:], acc[:], 0.04, old_s[:, b, :], ALU.mult, ALU.max)
-            nc.sync.dma_start(out[b * P : (b + 1) * P, :], res[:])
+                for h in range(parts):
+                    cols = slice(h * width, (h + 1) * width)
+                    nc.tensor.matmul_mx(
+                        accs[h][:],
+                        lhsT=u_codes[b, a][:].bitcast(E4M3),
+                        lhsT_scale=u_scales[b, a][:],
+                        rhs=g_codes[a][:, cols].bitcast(E5M2),
+                        rhs_scale=g_scales[a][:, cols],
+                        start=(a == 0),
+                        stop=(a == PASSES - 1),
+                    )
+            for h in range(parts):
+                cols = slice(h * width, (h + 1) * width)
+                res = keep.tile([P, width], F32, name="res%d%d" % (b, h))
+                nc.vector.scalar_tensor_tensor(res[:], accs[h][:], 0.04, old_s[:, b, cols], ALU.mult, ALU.max)
+                nc.sync.dma_start(out[b * P : (b + 1) * P, cols], res[:])

from contextlib import ExitStack

import concourse.mybir as mybir

K, J, N, T = 256, 1024, 256, 2048
FLOPS = 2 * K * J * N

F32 = mybir.dt.float32
BF16 = mybir.dt.bfloat16
U32 = mybir.dt.uint32
U16 = mybir.dt.uint16
U8 = mybir.dt.uint8
E4M3 = mybir.dt.float8_e4m3fn_x4
E5M2 = mybir.dt.float8_e5m2_x4
ALU = mybir.AluOpType
ACT = mybir.ActivationFunctionType
AX = mybir.AxisListType

P = 128
QUAD = 32
PACK = 4
PASS = P * PACK
PASSES = J // PASS
BLOCKS = 2
LIST_COLS = PASS // 16
LAST = (BLOCKS - 1, PASSES - 1)


def tile_list_moment_products_sized_larger_kernel(tc, xf, ra, xb, gt, cb, old, offs, offs2, offs3, out):
    nc = tc.nc
    with ExitStack() as ctx:
        keep = ctx.enter_context(tc.tile_pool(name="keep", bufs=1))
        psum = ctx.enter_context(tc.psum_pool(name="psum", bufs=1))

        def load_list(src, name):
            t = keep.tile([P, J // 16], U16, name=name)
            nc.sync.dma_start(t[:], src)
            return t

        def load_rows(src, b, name):
            t = keep.tile([P, T], F32, name=name, align_bytes=64)
            nc.sync.dma_start(t[:], src[b * P : (b + 1) * P, :])
            return t

        ra_sb = keep.tile([P, J // P], F32, name="ra_sb")
        inv_pair = keep.tile([P, 2, PASSES, PACK], F32, name="inv_pair")
        nc.sync.dma_start(ra_sb[:], ra.rearrange("o (p c) -> (o p) c", p=P))
        g_tab = [load_rows(gt, 0, "g_tab0")]
        list_g = load_list(offs3, "list_g")
        g_tab.append(load_rows(gt, 1, "g_tab1"))
        list_f = load_list(offs, "list_f")
        f_tab = [load_rows(xf, b, "f_tab%d" % b) for b in range(BLOCKS)]
        nc.sync.dma_start(inv_pair[:, 1], cb.rearrange("(a p t) o -> p a (t o)", a=PASSES, t=PACK))
        list_b = load_list(offs2, "list_b")
        b_tab = [load_rows(xb, b, "b_tab%d" % b) for b in range(BLOCKS)]
        old_sb = keep.tile([P, BLOCKS, N], F32, name="old_sb")
        nc.sync.dma_start(old_sb[:], old.rearrange("(b p) n -> p b n", p=P))

        ident = keep.tile([P, P], F32, name="ident")
        ones = keep.tile([P, P], F32, name="ones")
        col = keep.tile([P, P], F32, name="col", align_bytes=64)
        row = keep.tile([P, P], F32, name="row", align_bytes=64)
        nc.vector.memset(ones[:], 1.0)
        nc.vector.memset(ident[:], 0.0)
        nc.vector.tensor_tensor_scan(col[:], ones[:], ones[:], 0.0, ALU.mult, ALU.add)
        nc.vector.transpose(row[:], col[:])
        for q in range(P // QUAD):
            s = slice(QUAD * q, QUAD * (q + 1))
            nc.vector.tensor_tensor(ident[s, s], row[s, s], col[s, s], ALU.is_equal)
        warm = keep.tile([P, 1], F32, name="warm")
        nc.scalar.activation(warm[:], ones[:, 0:1], ACT.Abs)

        def picked(tab, lst, a):
            return tab[:].indirect(lst[:, a * LIST_COLS : (a + 1) * LIST_COLS])

        def gather_vector(tab, lst, a, name):
            t = keep.tile([P, PASS], F32, name=name)
            nc.vector.tensor_copy(t[:], picked(tab, lst, a))
            return t

        def gather_scalar(tab, lst, a, name):
            t = keep.tile([P, PASS], F32, name=name, align_bytes=64)
            nc.scalar.activation(t[:], picked(tab, lst, a), ACT.Copy)
            return t

        ra_spread = keep.tile([P, J], F32, name="ra_spread")
        for h in range(2):
            bank = psum.tile([P, PACK, P], F32, name="ra_bank%d" % h, tag="spare%d" % h)
            for c in range(PACK):
                column = ra_sb[:, PACK * h + c : PACK * h + c + 1]
                nc.tensor.transpose(bank[:, c, :], column.to_broadcast([P, P]), ident[:])
            nc.scalar.activation(
                ra_spread[:].rearrange("p (q h c) -> p h q c", h=2, c=PACK)[:, h],
                bank[:].rearrange("p c q -> p q c"),
                ACT.Copy,
            )
        ra_all = [ra_spread[:, a * PASS : (a + 1) * PASS] for a in range(PASSES)]

        g_t = {}
        for b in range(BLOCKS):
            rows = [gather_vector(g_tab[b], list_g, 0, "g_rows0%d" % b), gather_scalar(g_tab[b], list_g, 1, "g_rows1%d" % b)]
            for a in range(PASSES):
                bank = psum.tile([P, PACK, P], F32, name="g_t%d%d" % (a, b))
                for t in range(PACK):
                    nc.tensor.transpose(bank[:, t, :], rows[a][:, t:PASS:PACK], ident[:])
                g_t[a, b] = bank

        g_abs = keep.tile([P, PASSES, PACK, N], F32, name="g_abs", tag="g_tab1", align_bytes=64)
        for b in range(BLOCKS):
            for a in range(PASSES):
                nc.scalar.activation(g_abs[:, a, :, b * P : (b + 1) * P], g_t[a, b][:], ACT.Abs)

        f_w = {}
        f_first = keep.tile([P, J], F32, name="f_first")
        nc.vector.tensor_tensor(f_first[:], f_tab[0][:].indirect(list_f[:]), ra_spread[:], ALU.mult)
        for a in range(PASSES):
            f_w[0, a] = f_first[:, a * PASS : (a + 1) * PASS]

        max_pair = keep.tile([P, PASSES, PACK, 2], F32, name="max_pair", tag="f_tab0", align_bytes=64)
        nc.vector.tensor_scalar(max_pair[:, :, :, 1], ones[:, 0 : PASSES * PACK].rearrange("p (a t) -> p a t", t=PACK), 0.2, None, ALU.mult)
        fac = []
        for a in range(PASSES):
            den = keep.tile([P, PACK], F32, name="den%d" % a)
            fac.append(keep.tile([P, PACK], F32, name="fac%d" % a))
            nc.vector.tensor_reduce(max_pair[:, a, :, 0], g_abs[:, a], AX.X, ALU.max)
            nc.vector.tensor_reduce(den[:], max_pair[:, a], AX.X, ALU.add)
            nc.vector.reciprocal(inv_pair[:, 0, a], den[:])
            nc.vector.tensor_reduce(fac[a][:], inv_pair[:, :, a].rearrange("p s t -> p t s"), AX.X, ALU.mult)

        g_bf = []
        for a in range(PASSES):
            g_bf.append(keep.tile([P, N, PACK], BF16, name="g_bf%d" % a, align_bytes=64))
            for b in range(BLOCKS):
                nc.vector.tensor_tensor(
                    g_bf[a][:, b * P : (b + 1) * P, :],
                    g_t[a, b][:].rearrange("p t n -> p n t"),
                    fac[a][:].unsqueeze(1).to_broadcast([P, P, PACK]),
                    ALU.mult,
                )

        for a in range(PASSES):
            plain = gather_scalar(f_tab[1], list_f, a, "f_rows%d" % a)
            weighted = keep.tile([P, PASS], F32, name="f_w1%d" % a)
            nc.gpsimd.tensor_tensor(weighted[:], plain[:], ra_all[a], ALU.mult)
            f_w[1, a] = weighted[:]

        g_codes = []
        g_scales = []

        def quantize_gradients(a, slot):
            g_codes.append(keep.tile([P, N], U32, name="g_codes%d" % a, tag=slot, align_bytes=64))
            g_scales.append(keep.tile([P, N], U8, name="g_scales%d" % a, align_bytes=64))
            nc.vector.quantize_mx(g_codes[a][:].bitcast(E5M2), g_scales[a][:], g_bf[a][:].rearrange("p n t -> p (n t)"))

        quantize_gradients(0, "g_codes0")

        prod = {}
        for b in range(BLOCKS):
            for a in range(PASSES):
                prod[b, a] = keep.tile([P, PASS], BF16, name="prod%d%d" % (b, a))
                engine = nc.gpsimd if (b, a) == (0, 0) else nc.vector
                parts = 2 if (b, a) == LAST else 1
                width = PASS // parts
                for h in range(parts):
                    rows_b = keep.tile([P, width], F32, name="b_rows%d%d%d" % (b, a, h), align_bytes=64)
                    first = (a * PASS + h * width) // 16
                    nc.scalar.activation(rows_b[:], b_tab[b][:].indirect(list_b[:, first : first + width // 16]), ACT.Copy)
                    cols = slice(h * width, (h + 1) * width)
                    engine.tensor_tensor(prod[b, a][:, cols], rows_b[:], f_w[b, a][:, cols], ALU.mult)

        quantize_gradients(1, "b_rows100")

        old_s = keep.tile([P, BLOCKS, N], F32, name="old_s", tag="b_rows111", align_bytes=64)
        nc.vector.tensor_scalar(old_s[:], old_sb[:], 0.04, None, ALU.mult)

        grouped_lo = keep.tile([P, PASSES, PASS], BF16, name="grouped_lo", tag="b_tab1", align_bytes=64)
        grouped_hi = keep.tile([P, PASSES, PASS], BF16, name="grouped_hi", align_bytes=64)
        u_codes = {}
        u_scales = {}
        for b in range(BLOCKS):
            for a in range(PASSES):
                words = prod[b, a][:].bitcast(F32)
                bank = psum.tile([P, 2, P], F32, name="u_t%d%d" % (b, a), tag=("spare%d" % a) if b == 0 else ("g_t%d0" % a))
                for u in range(2):
                    nc.tensor.transpose(bank[:, u, :], words[:, u : 2 * P : 2], ident[:])
                u_codes[b, a] = keep.tile([P, P], U32, name="u_codes%d%d" % (b, a), align_bytes=64)
                u_scales[b, a] = keep.tile([P, P], U8, name="u_scales%d%d" % (b, a), align_bytes=64)
                parts = 2 if (b, a) == LAST else 1
                width = P // parts
                for h in range(parts):
                    cols = slice(h * width, (h + 1) * width)
                    grouped = (grouped_lo, grouped_hi)[b][:, a, PACK * h * width : PACK * (h + 1) * width]
                    nc.scalar.copy(grouped.bitcast(F32).rearrange("p (k u) -> p k u", u=2), bank[:, :, cols].rearrange("p u k -> p k u"))
                    nc.vector.quantize_mx(u_codes[b, a][:, cols].bitcast(E4M3), u_scales[b, a][:, cols], grouped)

        for b in range(BLOCKS):
            parts = 2 if b == BLOCKS - 1 else 1
            width = N // parts
            accs = [psum.tile([P, width], F32, name="acc%d%d" % (b, h), tag=("acc%d" % b, "g_t01")[h]) for h in range(parts)]
            for a in range(PASSES):
                for h in range(parts):
                    cols = slice(h * width, (h + 1) * width)
                    nc.tensor.matmul_mx(
                        accs[h][:],
                        lhsT=u_codes[b, a][:].bitcast(E4M3),
                        lhsT_scale=u_scales[b, a][:],
                        rhs=g_codes[a][:, cols].bitcast(E5M2),
                        rhs_scale=g_scales[a][:, cols],
                        start=(a == 0),
                        stop=(a == PASSES - 1),
                    )
            for h in range(parts):
                cols = slice(h * width, (h + 1) * width)
                res = keep.tile([P, width], F32, name="res%d%d" % (b, h))
                nc.vector.scalar_tensor_tensor(res[:], accs[h][:], 0.04, old_s[:, b, cols], ALU.mult, ALU.max)
                nc.sync.dma_start(out[b * P : (b + 1) * P, cols], res[:])
